import numpy as np
import ml_dtypes


def mxq(x, axis, fmt="e4m3"):
    dtype, down = {"e4m3": (ml_dtypes.float8_e4m3fn, 7), "e5m2": (ml_dtypes.float8_e5m2, 14)}[fmt]
    v = np.moveaxis(np.asarray(x, np.float32).astype(ml_dtypes.bfloat16).astype(np.float64), axis, -1)
    blocks = v.reshape(v.shape[:-1] + (-1, 32))
    amax = np.abs(blocks).max(-1, keepdims=True)
    byte = np.maximum(np.where(amax > 0, np.frexp(amax)[1] - 1 + 127, 0) - down, 1)
    scale = np.exp2(byte - 127.0)
    codes = (blocks / scale).astype(np.float32).astype(dtype).astype(np.float64)
    return np.moveaxis((codes * scale).reshape(v.shape), -1, axis)


WIDE = False


def mx_kscale(k):
    if not WIDE:
        return np.ones(k)
    levels = np.array([10, -10, 5, -5, 0])
    if k % 512:
        return np.exp2(np.random.permutation(np.resize(levels, k // 32))).repeat(32)
    a = np.empty((k // 512, 16))
    for p in range(k // 512):
        a[p, :8] = np.random.permutation(np.resize(levels, 8))
        for g in range(8):
            far = levels[np.abs(levels - a[p, g]) >= 10]
            a[p, g + 8] = far[np.random.randint(len(far))]
    return np.exp2(a.ravel()).repeat(32)


def f64(x):
    return np.asarray(x).astype(np.float64)


def striped(idx):
    return np.tile(idx.reshape(-1, 16).T, (8, 1)).astype(np.uint16)


def unstriped(offs):
    return offs[:16].T.reshape(-1).astype(np.int64)


E2M1 = np.array([0.0, 0.5, 1.0, 1.5, 2.0, 3.0, 4.0, 6.0, -0.0, -0.5, -1.0, -1.5, -2.0, -3.0, -4.0, -6.0])


def pack_weight(w, fmt):
    k, n = w.shape
    w = f64(np.asarray(w, np.float32).astype(ml_dtypes.bfloat16)).reshape(k // 32, 32, n)
    amax = np.abs(w).max(1)
    if fmt == "e4m3":
        byte = np.frexp(amax)[1] - 1 + 127 - 7
    else:
        mant, ex = np.frexp(amax / 6.0)
        byte = np.where(mant > 0.5, ex, ex - 1) + 127
    byte = np.clip(np.where(amax > 0, byte, 1), 1, 254)
    scaled = (w * np.exp2(127.0 - byte)[:, None, :]).reshape(k, n).astype(np.float32)
    by_word = np.ascontiguousarray(scaled.reshape(k // 512, 128, 4, n).transpose(0, 1, 3, 2))
    if fmt == "e4m3":
        words = by_word.astype(ml_dtypes.float8_e4m3fn).view(np.uint8)
    else:
        c = by_word.astype(ml_dtypes.float4_e2m1fn).view(np.uint8) & 0xF
        words = (c[..., 0::2] | (c[..., 1::2] << 4)).reshape(k // 512, 128, 2 * n)
    return np.ascontiguousarray(words), np.ascontiguousarray(byte.astype(np.uint8).reshape(k // 512, 16, n))


def unpack_weight(words, scales, fmt):
    g, _, n = scales.shape
    words = np.ascontiguousarray(words).reshape(g, 128, n, -1)
    if fmt == "e4m3":
        vals = words.view(ml_dtypes.float8_e4m3fn).astype(np.float64)
    else:
        nib = np.empty((g, 128, n, 4), np.uint8)
        nib[..., 0::2] = words & 0xF
        nib[..., 1::2] = words >> 4
        vals = E2M1[nib]
    vals = vals * np.repeat(np.exp2(scales.astype(np.float64) - 127.0), 8, axis=1)[..., None]
    return vals.transpose(0, 1, 3, 2).reshape(g * 512, n)


def pack_table4(v):
    words, scales = pack_weight(v, "e2m1")
    g, t = words.shape[0] // 2, v.shape[1]
    words = words.reshape(g, 2, 128, t, 2).transpose(0, 2, 3, 1, 4)
    return np.concatenate([words.reshape(g, -1), scales.reshape(g, -1)], axis=1)


def unpack_table4(tab):
    g, t = tab.shape[0], tab.shape[1] // 544
    words = tab[:, :512 * t].reshape(g, 128, t, 2, 2).transpose(0, 3, 1, 2, 4).reshape(2 * g, 128, 2 * t)
    return unpack_weight(words, tab[:, 512 * t:].reshape(2 * g, 16, t), "e2m1")


def pack_table(v):
    words, scales = pack_weight(v, "e4m3")
    return np.concatenate([words.reshape(words.shape[0], -1), scales.reshape(scales.shape[0], -1)], axis=1)


def unpack_table(tab):
    g, t = tab.shape[0], tab.shape[1] // 528
    return unpack_weight(tab[:, :512 * t].reshape(g, 128, t, 4), tab[:, 512 * t:].reshape(g, 16, t), "e4m3")


def silu(v):
    return v / (1.0 + np.exp(-np.maximum(v, -700.0)))


K, L, M, T, S = 1536, 2048, 256, 1024, 256


def setup_inputs():
    n = np.random.standard_normal
    s1 = mx_kscale(K)[:, None]
    s2 = mx_kscale(L)[:, None]
    p_w4 = pack_weight(n((K, M)) / np.sqrt(K) / s1, "e2m1")
    return {
        "tab": pack_table(n((K, T)) * s1),
        "w4_words": p_w4[0],
        "w4_scales": p_w4[1],
        "tab2": pack_table4(n((L, T)) * s2),
        "u": (n((L, M)) / np.sqrt(L) / s2).astype(np.float32),
        "b": (0.3 * n(256)).astype(np.float32),
        "offs": striped(np.random.permutation(T)[:S]),
        "offs2": striped(np.random.permutation(T)[:S]),
    }


def reference(tab, w4_words, w4_scales, tab2, u, b, offs, offs2):
    tab_ = unpack_table(tab)[:, unstriped(offs)]
    w4_ = unpack_weight(w4_words, w4_scales, "e2m1")
    tab2_ = unpack_table4(tab2)[:, unstriped(offs2)]
    u_ = mxq(f64(u), 0, "e4m3")
    y = w4_.T @ tab_ + u_.T @ tab2_
    return silu(y + f64(b)[:, None])

@@ -1,0 +1,182 @@
+from contextlib import ExitStack
+
+import concourse.mybir as mybir
+
+K, L, M, T, S = 1536, 2048, 256, 1024, 256
+FLOPS = 2 * (K + L) * M * S
+
+F32 = mybir.dt.float32
+BF16 = mybir.dt.bfloat16
+I32 = mybir.dt.int32
+U32 = mybir.dt.uint32
+U16 = mybir.dt.uint16
+U8 = mybir.dt.uint8
+E4M3X4 = mybir.dt.float8_e4m3fn_x4
+E2M1X4 = mybir.dt.float4_e2m1fn_x4
+ACT = mybir.ActivationFunctionType
+
+P = 128
+KP = K // 512
+LP = L // 512
+LM = LP // 2
+H = 128
+
+
+def tile_list_tab48_silu_kernel(
+    tc, tab, w4_words, w4_scales, tab2, u, b, offs, offs2, out
+):
+    nc = tc.nc
+    with ExitStack() as ctx:
+        keep = ctx.enter_context(tc.tile_pool(name="keep", bufs=1))
+        psum = ctx.enter_context(tc.psum_pool(name="psum", bufs=1))
+
+        list1 = keep.tile([P, S // 16], U16, name="list1")
+        list2 = keep.tile([P, S // 16], U16, name="list2")
+        words1 = [keep.tile([P, T], I32, name=f"words1_{a}", align_bytes=64) for a in range(KP)]
+        words2 = [keep.tile([P, T], I32, name=f"words2_{m}", align_bytes=64) for m in range(LM)]
+        plane1 = keep.tile([P, KP, T], U8, name="plane1", align_bytes=64)
+        plane2 = [keep.tile([P, 2, T], U8, name=f"plane2_{m}", align_bytes=64) for m in range(LM)]
+        w_codes = keep.tile([P, KP, 2 * M], U8, name="w_codes", align_bytes=64)
+        w_plane = keep.tile([P, KP, M], U8, name="w_plane", align_bytes=64)
+        raw = [keep.tile([P, 4, M], F32, name=f"raw_{c}", align_bytes=64) for c in range(LP)]
+        mixed = [keep.tile([P, M, 4], BF16, name=f"mixed_{c}", align_bytes=64) for c in range(LP)]
+        u_codes = [keep.tile([P, M], U32, name=f"u_codes_{c}", align_bytes=64) for c in range(LP)]
+        u_plane = [keep.tile([P, M], U8, name=f"u_plane_{c}", align_bytes=64) for c in range(LP)]
+        got1 = [keep.tile([P, S], U32, name=f"got1_{a}", align_bytes=64) for a in range(KP)]
+        gots1 = [keep.tile([P, S], U8, name=f"gots1_{a}", align_bytes=64) for a in range(KP)]
+        got2 = [keep.tile([P, S], U32, name=f"got2_{m}", align_bytes=64) for m in range(LM)]
+        gots2 = [keep.tile([P, S], U8, name=f"gots2_{c}", align_bytes=64) for c in range(LP)]
+        part2 = [keep.tile([P, 2, 2 * S], U8, name=f"part2_{m}", align_bytes=64) for m in range(LM)]
+        bias = keep.tile([P, M // P], F32, name="bias")
+        warm = keep.tile([P, 1], F32, name="warm")
+        res = [keep.tile([P, M // P, H], F32, name=f"res_{h}", align_bytes=64) for h in range(2)]
+        acc = [[psum.tile([P, H], F32, name=f"acc_{n}_{h}") for h in range(2)] for n in range(2)]
+
+        nc.vector.memset(warm[:], 0.0)
+        nc.scalar.activation(warm[:], warm[:], ACT.Silu)
+        for m in range(LM):
+            nc.vector.memset(plane2[m][:].rearrange("p h t -> p (h t)").bitcast(I32), 0)
+        nc.gpsimd.memset(w_plane[:].rearrange("p a n -> p (a n)").bitcast(I32), 0)
+        nc.vector.memset(plane1[:].rearrange("p a t -> p (a t)").bitcast(I32), 0)
+
+        def load_words(tile, row):
+            nc.sync.dma_start(tile[:], row[0 : 512 * T].rearrange("(p b) -> p b", p=P).bitcast(I32))
+
+        def load_u(c):
+            nc.sync.dma_start(raw[c][:], u[512 * c : 512 * (c + 1), :].rearrange("(p j) n -> p j n", j=4))
+
+        def load_plane2(m):
+            rows = tab2[m, 512 * T : 544 * T].rearrange("(h q t) -> q h t", h=2, q=16)
+            for r in range(4):
+                nc.sync.dma_start(plane2[m][r:P:32].bitcast(I32), rows[r:16:4].bitcast(I32))
+
+        def load_plane1():
+            rows = tab[:, 512 * T : 528 * T].rearrange("a (q t) -> q a t", q=16)
+            for r in range(4):
+                nc.sync.dma_start(plane1[r:P:32].bitcast(I32), rows[r:16:4].bitcast(I32))
+
+        nc.sync.dma_start(list2[:], offs2)
+        nc.sync.dma_start(list1[:], offs)
+        load_words(words2[0], tab2[0])
+        load_plane2(0)
+        load_u(0)
+        load_words(words2[1], tab2[1])
+        load_plane2(1)
+        load_u(1)
+        load_words(words1[0], tab[0])
+        load_plane1()
+        load_u(2)
+        nc.sync.dma_start(w_codes[:].bitcast(I32), w4_words.rearrange("a p n -> p a n").bitcast(I32))
+        load_words(words1[1], tab[1])
+        load_u(3)
+        load_words(words1[2], tab[2])
+        w_rows = w4_scales.rearrange("a q n -> q a n")
+        for r in range(4):
+            nc.gpsimd.dma_start(w_plane[r:P:32].bitcast(I32), w_rows[r:16:4].bitcast(I32))
+        with nc.allow_non_contiguous_dma(reason="one bias value to a partition"):
+            nc.gpsimd.dma_start(bias[:], b.rearrange("(n p) -> p n", p=P))
+
+        passes = 0
+        total = KP + LP
+
+        def multiply(lhs, lhs_scale, rhs, rhs_scale, first, last, order):
+            for h in range(2):
+                for n in range(2):
+                    nc.tensor.matmul_mx(
+                        out=acc[n][h][:],
+                        lhsT=lhs(n),
+                        lhsT_scale=lhs_scale[:, n * P : (n + 1) * P],
+                        rhs=rhs(h),
+                        rhs_scale=rhs_scale[:, h * H : (h + 1) * H],
+                        start=first,
+                        stop=last,
+                    )
+
+        def gather(dst, window, lst, lo=0, hi=S):
+            idx = lst[:] if (lo, hi) == (0, S) else lst[:, lo // 16 : hi // 16]
+            nc.vector.tensor_copy(dst[:, lo:hi], window.indirect(idx))
+
+        def mix(c):
+            nc.scalar.copy(mixed[c][:], raw[c][:].rearrange("p j n -> p n j"))
+
+        def quantise(c):
+            nc.vector.quantize_mx(
+                out=u_codes[c][:].bitcast(E4M3X4),
+                scales=u_plane[c][:],
+                in_=mixed[c][:].rearrange("p n j -> p (n j)"),
+            )
+
+        def table2(m):
+            gather(got2[m], words2[m][:].bitcast(U32), list2)
+            for h in range(2):
+                gather(gots2[2 * m + h], plane2[m][:, h, :], list2)
+            nc.vector.tensor_copy(
+                part2[m][:].rearrange("p h b -> p (h b)").bitcast(U16).rearrange("p (h t) -> p h t", h=2),
+                got2[m][:].bitcast(U16).rearrange("p (t h) -> p h t", h=2),
+            )
+
+        def u_pass(c, first):
+            multiply(
+                lambda n: u_codes[c][:, n * P : (n + 1) * P].bitcast(E4M3X4),
+                u_plane[c],
+                lambda h: part2[c // 2][:, c % 2, 2 * h * H : 2 * (h + 1) * H].bitcast(E2M1X4),
+                gots2[c],
+                first, False, None,
+            )
+
+        def w_pass(a, last):
+            multiply(
+                lambda n: w_codes[:, a, 2 * n * P : 2 * (n + 1) * P].bitcast(E2M1X4),
+                w_plane[:, a, :],
+                lambda h: got1[a][:, h * H : (h + 1) * H].bitcast(E4M3X4),
+                gots1[a],
+                False, last, None,
+            )
+
+        table2(0)
+        mix(0)
+        quantise(0)
+        u_pass(0, True)
+        table2(1)
+        mix(1)
+        quantise(1)
+        u_pass(1, False)
+        for a in range(KP):
+            gather(gots1[a], plane1[:, a, :], list1)
+        gather(got1[0], words1[0][:].bitcast(U32), list1)
+        mix(2)
+        quantise(2)
+        u_pass(2, False)
+        w_pass(0, False)
+        gather(got1[1], words1[1][:].bitcast(U32), list1)
+        mix(3)
+        quantise(3)
+        u_pass(3, False)
+        w_pass(1, False)
+        for h in range(2):
+            gather(got1[2], words1[2][:].bitcast(U32), list1, h * H, (h + 1) * H)
+        w_pass(2, True)
+        for h in range(2):
+            for n in range(2):
+                nc.scalar.activation(res[h][:, n, :], acc[n][h][:], ACT.Silu, bias=bias[:, n : n + 1])
+            nc.sync.dma_start(out[:, h * H : (h + 1) * H].rearrange("(n p) j -> p n j", p=P), res[h][:])

@@ -54,10 +54,10 @@ def tile_list_tab48_silu_kernel(
 
         nc.vector.memset(warm[:], 0.0)
         nc.scalar.activation(warm[:], warm[:], ACT.Silu)
-        for m in range(LM):
-            nc.vector.memset(plane2[m][:].rearrange("p h t -> p (h t)").bitcast(I32), 0)
-        nc.gpsimd.memset(w_plane[:].rearrange("p a n -> p (a n)").bitcast(I32), 0)
+        nc.vector.memset(plane2[0][:].rearrange("p h t -> p (h t)").bitcast(I32), 0)
+        nc.vector.memset(w_plane[:].rearrange("p a n -> p (a n)").bitcast(I32), 0)
         nc.vector.memset(plane1[:].rearrange("p a t -> p (a t)").bitcast(I32), 0)
+        nc.vector.memset(plane2[1][:].rearrange("p h t -> p (h t)").bitcast(I32), 0)
 
         def load_words(tile, row):
             nc.sync.dma_start(tile[:], row[0 : 512 * T].rearrange("(p b) -> p b", p=P).bitcast(I32))
@@ -77,24 +77,24 @@ def tile_list_tab48_silu_kernel(
 
         nc.sync.dma_start(list2[:], offs2)
         nc.sync.dma_start(list1[:], offs)
+        with nc.allow_non_contiguous_dma(reason="one bias value to a partition"):
+            nc.scalar.dma_start(bias[:], b.rearrange("(n p) -> p n", p=P))
         load_words(words2[0], tab2[0])
         load_plane2(0)
         load_u(0)
+        load_plane1()
         load_words(words2[1], tab2[1])
         load_plane2(1)
         load_u(1)
         load_words(words1[0], tab[0])
-        load_plane1()
         load_u(2)
-        nc.sync.dma_start(w_codes[:].bitcast(I32), w4_words.rearrange("a p n -> p a n").bitcast(I32))
-        load_words(words1[1], tab[1])
-        load_u(3)
-        load_words(words1[2], tab[2])
         w_rows = w4_scales.rearrange("a q n -> q a n")
         for r in range(4):
-            nc.gpsimd.dma_start(w_plane[r:P:32].bitcast(I32), w_rows[r:16:4].bitcast(I32))
-        with nc.allow_non_contiguous_dma(reason="one bias value to a partition"):
-            nc.gpsimd.dma_start(bias[:], b.rearrange("(n p) -> p n", p=P))
+            nc.sync.dma_start(w_plane[r:P:32].bitcast(I32), w_rows[r:16:4].bitcast(I32))
+        load_u(3)
+        nc.sync.dma_start(w_codes[:].bitcast(I32), w4_words.rearrange("a p n -> p a n").bitcast(I32))
+        load_words(words1[1], tab[1])
+        load_words(words1[2], tab[2])
 
         passes = 0
         total = KP + LP
@@ -128,8 +128,6 @@ def tile_list_tab48_silu_kernel(
 
         def table2(m):
             gather(got2[m], words2[m][:].bitcast(U32), list2)
-            for h in range(2):
-                gather(gots2[2 * m + h], plane2[m][:, h, :], list2)
             nc.vector.tensor_copy(
                 part2[m][:].rearrange("p h b -> p (h b)").bitcast(U16).rearrange("p (h t) -> p h t", h=2),
                 got2[m][:].bitcast(U16).rearrange("p (t h) -> p h t", h=2),
@@ -153,25 +151,34 @@ def tile_list_tab48_silu_kernel(
                 False, last, None,
             )
 
+        def table2_planes(m):
+            for h in range(2):
+                gather(gots2[2 * m + h], plane2[m][:, h, :], list2)
+
+        def words_of_table1(a):
+            gather(got1[a], words1[a][:].bitcast(U32), list1)
+
         table2(0)
+        table2_planes(0)
         mix(0)
         quantise(0)
         u_pass(0, True)
+        for a in range(KP):
+            gather(gots1[a], plane1[:, a, :], list1)
         table2(1)
+        table2_planes(1)
         mix(1)
         quantise(1)
         u_pass(1, False)
-        for a in range(KP):
-            gather(gots1[a], plane1[:, a, :], list1)
-        gather(got1[0], words1[0][:].bitcast(U32), list1)
+        words_of_table1(0)
         mix(2)
         quantise(2)
         u_pass(2, False)
-        w_pass(0, False)
-        gather(got1[1], words1[1][:].bitcast(U32), list1)
         mix(3)
         quantise(3)
         u_pass(3, False)
+        w_pass(0, False)
+        words_of_table1(1)
         w_pass(1, False)
         for h in range(2):
             gather(got1[2], words1[2][:].bitcast(U32), list1, h * H, (h + 1) * H)
@@ -179,4 +186,5 @@ def tile_list_tab48_silu_kernel(
         for h in range(2):
             for n in range(2):
                 nc.scalar.activation(res[h][:, n, :], acc[n][h][:], ACT.Silu, bias=bias[:, n : n + 1])
-            nc.sync.dma_start(out[:, h * H : (h + 1) * H].rearrange("(n p) j -> p n j", p=P), res[h][:])
+                store = nc.sync if n == 0 else nc.scalar
+                store.dma_start(out[n * P : (n + 1) * P, h * H : (h + 1) * H], res[h][:, n, :])

@@ -47,7 +47,8 @@ def tile_list_tab48_silu_kernel(
         got2 = [keep.tile([P, S], U32, name=f"got2_{m}", align_bytes=64) for m in range(LM)]
         gots2 = [keep.tile([P, S], U8, name=f"gots2_{c}", align_bytes=64) for c in range(LP)]
         part2 = [keep.tile([P, 2, 2 * S], U8, name=f"part2_{m}", align_bytes=64) for m in range(LM)]
-        bias = keep.tile([P, M // P], F32, name="bias")
+        bias_rows = keep.tile([P, P], F32, name="bias_rows", align_bytes=64)
+        bias = keep.tile([P, P], F32, name="bias", align_bytes=64)
         warm = keep.tile([P, 1], F32, name="warm")
         res = [keep.tile([P, M // P, H], F32, name=f"res_{h}", align_bytes=64) for h in range(2)]
         acc = [[psum.tile([P, H], F32, name=f"acc_{n}_{h}") for h in range(2)] for n in range(2)]
@@ -55,9 +56,10 @@ def tile_list_tab48_silu_kernel(
         nc.vector.memset(warm[:], 0.0)
         nc.scalar.activation(warm[:], warm[:], ACT.Silu)
         nc.vector.memset(plane2[0][:].rearrange("p h t -> p (h t)").bitcast(I32), 0)
-        nc.vector.memset(w_plane[:].rearrange("p a n -> p (a n)").bitcast(I32), 0)
+        nc.gpsimd.memset(bias_rows[:], 0.0)
         nc.vector.memset(plane1[:].rearrange("p a t -> p (a t)").bitcast(I32), 0)
         nc.vector.memset(plane2[1][:].rearrange("p h t -> p (h t)").bitcast(I32), 0)
+        nc.vector.memset(w_plane[:].rearrange("p a n -> p (a n)").bitcast(I32), 0)
 
         def load_words(tile, row):
             nc.sync.dma_start(tile[:], row[0 : 512 * T].rearrange("(p b) -> p b", p=P).bitcast(I32))
@@ -65,36 +67,39 @@ def tile_list_tab48_silu_kernel(
         def load_u(c):
             nc.sync.dma_start(raw[c][:], u[512 * c : 512 * (c + 1), :].rearrange("(p j) n -> p j n", j=4))
 
-        def load_plane2(m):
-            rows = tab2[m, 512 * T : 544 * T].rearrange("(h q t) -> q h t", h=2, q=16)
-            for r in range(4):
-                nc.sync.dma_start(plane2[m][r:P:32].bitcast(I32), rows[r:16:4].bitcast(I32))
+        rows2 = [tab2[m, 512 * T : 544 * T].rearrange("(h q t) -> q h t", h=2, q=16) for m in range(LM)]
+        rows1 = tab[:, 512 * T : 528 * T].rearrange("a (q t) -> q a t", q=16)
+        rows_w = w4_scales.rearrange("a q n -> q a n")
 
-        def load_plane1():
-            rows = tab[:, 512 * T : 528 * T].rearrange("a (q t) -> q a t", q=16)
-            for r in range(4):
-                nc.sync.dma_start(plane1[r:P:32].bitcast(I32), rows[r:16:4].bitcast(I32))
+        def load_rows(plane, rows, which):
+            for r in which:
+                nc.sync.dma_start(plane[r:P:32].bitcast(I32), rows[r:16:4].bitcast(I32))
 
-        nc.sync.dma_start(list2[:], offs2)
-        nc.sync.dma_start(list1[:], offs)
-        with nc.allow_non_contiguous_dma(reason="one bias value to a partition"):
-            nc.scalar.dma_start(bias[:], b.rearrange("(n p) -> p n", p=P))
+        def load_w(lo, hi):
+            nc.sync.dma_start(w_codes[:, lo:hi].bitcast(I32), w4_words[lo:hi].rearrange("a p n -> p a n").bitcast(I32))
+
         load_words(words2[0], tab2[0])
-        load_plane2(0)
+        nc.sync.dma_start(list2[:], offs2)
+        load_rows(plane2[0], rows2[0], (0, 1))
         load_u(0)
-        load_plane1()
+        load_rows(plane2[0], rows2[0], (2, 3))
         load_words(words2[1], tab2[1])
-        load_plane2(1)
+        nc.sync.dma_start(list1[:], offs)
+        load_rows(plane1, rows1, (0, 1))
         load_u(1)
+        load_rows(plane1, rows1, (2, 3))
         load_words(words1[0], tab[0])
+        load_rows(plane2[1], rows2[1], (0, 1))
         load_u(2)
-        w_rows = w4_scales.rearrange("a q n -> q a n")
-        for r in range(4):
-            nc.sync.dma_start(w_plane[r:P:32].bitcast(I32), w_rows[r:16:4].bitcast(I32))
+        load_rows(plane2[1], rows2[1], (2, 3))
         load_u(3)
-        nc.sync.dma_start(w_codes[:].bitcast(I32), w4_words.rearrange("a p n -> p a n").bitcast(I32))
+        load_rows(w_plane, rows_w, (0, 1))
+        nc.sync.dma_start(bias_rows[0:P:32, 0:64], b.rearrange("(n q i) -> q n i", n=2, i=32))
         load_words(words1[1], tab[1])
+        load_rows(w_plane, rows_w, (2, 3))
+        load_w(0, 2)
         load_words(words1[2], tab[2])
+        load_w(2, 3)
 
         passes = 0
         total = KP + LP
@@ -177,6 +182,7 @@ def tile_list_tab48_silu_kernel(
         mix(3)
         quantise(3)
         u_pass(3, False)
+        nc.vector.transpose(bias[:], bias_rows[:])
         w_pass(0, False)
         words_of_table1(1)
         w_pass(1, False)
@@ -185,6 +191,6 @@ def tile_list_tab48_silu_kernel(
         w_pass(2, True)
         for h in range(2):
             for n in range(2):
-                nc.scalar.activation(res[h][:, n, :], acc[n][h][:], ACT.Silu, bias=bias[:, n : n + 1])
+                nc.scalar.activation(res[h][:, n, :], acc[n][h][:], ACT.Silu, bias=bias[:, 32 * n : 32 * n + 1])
                 store = nc.sync if n == 0 else nc.scalar
                 store.dma_start(out[n * P : (n + 1) * P, h * H : (h + 1) * H], res[h][:, n, :])

@@ -53,11 +53,10 @@ def tile_list_tab48_silu_kernel(
         res = [keep.tile([P, M // P, H], F32, name=f"res_{h}", align_bytes=64) for h in range(2)]
         acc = [[psum.tile([P, H], F32, name=f"acc_{n}_{h}") for h in range(2)] for n in range(2)]
 
-        nc.vector.memset(warm[:], 0.0)
-        nc.scalar.activation(warm[:], warm[:], ACT.Silu)
-        nc.vector.memset(plane2[0][:].rearrange("p h t -> p (h t)").bitcast(I32), 0)
+        nc.vector.memset(plane1[:, 0:2].rearrange("p a t -> p (a t)").bitcast(I32), 0)
+        nc.gpsimd.memset(plane1[:, 2].bitcast(I32), 0)
         nc.gpsimd.memset(bias_rows[:], 0.0)
-        nc.vector.memset(plane1[:].rearrange("p a t -> p (a t)").bitcast(I32), 0)
+        nc.vector.memset(plane2[0][:].rearrange("p h t -> p (h t)").bitcast(I32), 0)
         nc.vector.memset(plane2[1][:].rearrange("p h t -> p (h t)").bitcast(I32), 0)
         nc.vector.memset(w_plane[:].rearrange("p a n -> p (a n)").bitcast(I32), 0)
 
@@ -71,32 +70,31 @@ def tile_list_tab48_silu_kernel(
         rows1 = tab[:, 512 * T : 528 * T].rearrange("a (q t) -> q a t", q=16)
         rows_w = w4_scales.rearrange("a q n -> q a n")
 
-        def load_rows(plane, rows, which):
+        def load_rows(queue, plane, rows, which=range(4)):
             for r in which:
-                nc.sync.dma_start(plane[r:P:32].bitcast(I32), rows[r:16:4].bitcast(I32))
+                queue.dma_start(plane[r:P:32].bitcast(I32), rows[r:16:4].bitcast(I32))
 
         def load_w(lo, hi):
             nc.sync.dma_start(w_codes[:, lo:hi].bitcast(I32), w4_words[lo:hi].rearrange("a p n -> p a n").bitcast(I32))
 
+        nc.sync.dma_start(list1[:], offs)
+        load_rows(nc.sync, plane1, rows1)
         load_words(words2[0], tab2[0])
         nc.sync.dma_start(list2[:], offs2)
-        load_rows(plane2[0], rows2[0], (0, 1))
         load_u(0)
-        load_rows(plane2[0], rows2[0], (2, 3))
         load_words(words2[1], tab2[1])
-        nc.sync.dma_start(list1[:], offs)
-        load_rows(plane1, rows1, (0, 1))
+        load_rows(nc.sync, plane2[0], rows2[0], (0, 1))
         load_u(1)
-        load_rows(plane1, rows1, (2, 3))
+        load_rows(nc.sync, plane2[0], rows2[0], (2, 3))
         load_words(words1[0], tab[0])
-        load_rows(plane2[1], rows2[1], (0, 1))
-        load_u(2)
-        load_rows(plane2[1], rows2[1], (2, 3))
-        load_u(3)
-        load_rows(w_plane, rows_w, (0, 1))
         nc.sync.dma_start(bias_rows[0:P:32, 0:64], b.rearrange("(n q i) -> q n i", n=2, i=32))
+        load_rows(nc.sync, plane2[1], rows2[1], (0, 1))
+        load_u(2)
+        load_rows(nc.sync, plane2[1], rows2[1], (2, 3))
+        load_u(3)
+        load_rows(nc.sync, w_plane, rows_w, (0, 1))
         load_words(words1[1], tab[1])
-        load_rows(w_plane, rows_w, (2, 3))
+        load_rows(nc.sync, w_plane, rows_w, (2, 3))
         load_w(0, 2)
         load_words(words1[2], tab[2])
         load_w(2, 3)
@@ -122,7 +120,10 @@ def tile_list_tab48_silu_kernel(
             nc.vector.tensor_copy(dst[:, lo:hi], window.indirect(idx))
 
         def mix(c):
-            nc.scalar.copy(mixed[c][:], raw[c][:].rearrange("p j n -> p n j"))
+            nc.scalar.copy(
+                mixed[c][:].rearrange("p (c i) j -> p c j i", i=4),
+                raw[c][:].rearrange("p j (c i) -> p c j i", i=4),
+            )
 
         def quantise(c):
             nc.vector.quantize_mx(
@@ -163,26 +164,28 @@ def tile_list_tab48_silu_kernel(
         def words_of_table1(a):
             gather(got1[a], words1[a][:].bitcast(U32), list1)
 
+        nc.vector.memset(warm[:], 0.0)
+        nc.scalar.activation(warm[:], warm[:], ACT.Silu)
+        for a in range(KP):
+            gather(gots1[a], plane1[:, a, :], list1)
         table2(0)
         table2_planes(0)
         mix(0)
         quantise(0)
         u_pass(0, True)
-        for a in range(KP):
-            gather(gots1[a], plane1[:, a, :], list1)
         table2(1)
         table2_planes(1)
         mix(1)
         quantise(1)
         u_pass(1, False)
         words_of_table1(0)
+        nc.vector.transpose(bias[:], bias_rows[:])
         mix(2)
         quantise(2)
         u_pass(2, False)
         mix(3)
         quantise(3)
         u_pass(3, False)
-        nc.vector.transpose(bias[:], bias_rows[:])
         w_pass(0, False)
         words_of_table1(1)
         w_pass(1, False)

from contextlib import ExitStack

import concourse.mybir as mybir

K, L, M, T, S = 1536, 2048, 256, 1024, 256
FLOPS = 2 * (K + L) * M * S

F32 = mybir.dt.float32
BF16 = mybir.dt.bfloat16
I32 = mybir.dt.int32
U32 = mybir.dt.uint32
U16 = mybir.dt.uint16
U8 = mybir.dt.uint8
E4M3X4 = mybir.dt.float8_e4m3fn_x4
E2M1X4 = mybir.dt.float4_e2m1fn_x4
ACT = mybir.ActivationFunctionType

P = 128
KP = K // 512
LP = L // 512
LM = LP // 2
H = 128


def tile_list_tab48_silu_kernel(
    tc, tab, w4_words, w4_scales, tab2, u, b, offs, offs2, out
):
    nc = tc.nc
    with ExitStack() as ctx:
        keep = ctx.enter_context(tc.tile_pool(name="keep", bufs=1))
        psum = ctx.enter_context(tc.psum_pool(name="psum", bufs=1))

        list1 = keep.tile([P, S // 16], U16, name="list1")
        list2 = keep.tile([P, S // 16], U16, name="list2")
        words1 = [keep.tile([P, T], I32, name=f"words1_{a}", align_bytes=64) for a in range(KP)]
        words2 = [keep.tile([P, T], I32, name=f"words2_{m}", align_bytes=64) for m in range(LM)]
        plane1 = keep.tile([P, KP, T], U8, name="plane1", align_bytes=64)
        plane2 = [keep.tile([P, 2, T], U8, name=f"plane2_{m}", align_bytes=64) for m in range(LM)]
        w_codes = keep.tile([P, KP, 2 * M], U8, name="w_codes", align_bytes=64)
        w_plane = keep.tile([P, KP, M], U8, name="w_plane", align_bytes=64)
        raw = [keep.tile([P, 4, M], F32, name=f"raw_{c}", align_bytes=64) for c in range(LP)]
        mixed = [keep.tile([P, M, 4], BF16, name=f"mixed_{c}", align_bytes=64) for c in range(LP)]
        u_codes = [keep.tile([P, M], U32, name=f"u_codes_{c}", align_bytes=64) for c in range(LP)]
        u_plane = [keep.tile([P, M], U8, name=f"u_plane_{c}", align_bytes=64) for c in range(LP)]
        got1 = [keep.tile([P, S], U32, name=f"got1_{a}", align_bytes=64) for a in range(KP)]
        gots1 = [keep.tile([P, S], U8, name=f"gots1_{a}", align_bytes=64) for a in range(KP)]
        got2 = [keep.tile([P, S], U32, name=f"got2_{m}", align_bytes=64) for m in range(LM)]
        gots2 = [keep.tile([P, S], U8, name=f"gots2_{c}", align_bytes=64) for c in range(LP)]
        part2 = [keep.tile([P, 2, 2 * S], U8, name=f"part2_{m}", align_bytes=64) for m in range(LM)]
        bias_rows = keep.tile([P, P], F32, name="bias_rows", align_bytes=64)
        bias = keep.tile([P, P], F32, name="bias", align_bytes=64)
        warm = keep.tile([P, 1], F32, name="warm")
        res = [keep.tile([P, M // P, H], F32, name=f"res_{h}", align_bytes=64) for h in range(2)]
        acc = [[psum.tile([P, H], F32, name=f"acc_{n}_{h}") for h in range(2)] for n in range(2)]

        nc.vector.memset(plane1[:, 0:2].rearrange("p a t -> p (a t)").bitcast(I32), 0)
        nc.gpsimd.memset(plane1[:, 2].bitcast(I32), 0)
        nc.gpsimd.memset(bias_rows[:], 0.0)
        nc.vector.memset(plane2[0][:].rearrange("p h t -> p (h t)").bitcast(I32), 0)
        nc.vector.memset(plane2[1][:].rearrange("p h t -> p (h t)").bitcast(I32), 0)
        nc.vector.memset(w_plane[:].rearrange("p a n -> p (a n)").bitcast(I32), 0)

        def load_words(tile, row):
            nc.sync.dma_start(tile[:], row[0 : 512 * T].rearrange("(p b) -> p b", p=P).bitcast(I32))

        def load_u(c):
            nc.sync.dma_start(raw[c][:], u[512 * c : 512 * (c + 1), :].rearrange("(p j) n -> p j n", j=4))

        rows2 = [tab2[m, 512 * T : 544 * T].rearrange("(h q t) -> q h t", h=2, q=16) for m in range(LM)]
        rows1 = tab[:, 512 * T : 528 * T].rearrange("a (q t) -> q a t", q=16)
        rows_w = w4_scales.rearrange("a q n -> q a n")

        def load_rows(queue, plane, rows, which=range(4)):
            for r in which:
                queue.dma_start(plane[r:P:32].bitcast(I32), rows[r:16:4].bitcast(I32))

        def load_w(lo, hi):
            nc.sync.dma_start(w_codes[:, lo:hi].bitcast(I32), w4_words[lo:hi].rearrange("a p n -> p a n").bitcast(I32))

        nc.sync.dma_start(list1[:], offs)
        load_rows(nc.sync, plane1, rows1)
        load_words(words2[0], tab2[0])
        nc.sync.dma_start(list2[:], offs2)
        load_u(0)
        load_words(words2[1], tab2[1])
        load_rows(nc.sync, plane2[0], rows2[0], (0, 1))
        load_u(1)
        load_rows(nc.sync, plane2[0], rows2[0], (2, 3))
        load_words(words1[0], tab[0])
        nc.sync.dma_start(bias_rows[0:P:32, 0:64], b.rearrange("(n q i) -> q n i", n=2, i=32))
        load_rows(nc.sync, plane2[1], rows2[1], (0, 1))
        load_u(2)
        load_rows(nc.sync, plane2[1], rows2[1], (2, 3))
        load_u(3)
        load_rows(nc.sync, w_plane, rows_w, (0, 1))
        load_words(words1[1], tab[1])
        load_rows(nc.sync, w_plane, rows_w, (2, 3))
        load_w(0, 2)
        load_words(words1[2], tab[2])
        load_w(2, 3)

        passes = 0
        total = KP + LP

        def multiply(lhs, lhs_scale, rhs, rhs_scale, first, last, order):
            for h in range(2):
                for n in range(2):
                    nc.tensor.matmul_mx(
                        out=acc[n][h][:],
                        lhsT=lhs(n),
                        lhsT_scale=lhs_scale[:, n * P : (n + 1) * P],
                        rhs=rhs(h),
                        rhs_scale=rhs_scale[:, h * H : (h + 1) * H],
                        start=first,
                        stop=last,
                    )

        def gather(dst, window, lst, lo=0, hi=S):
            idx = lst[:] if (lo, hi) == (0, S) else lst[:, lo // 16 : hi // 16]
            nc.vector.tensor_copy(dst[:, lo:hi], window.indirect(idx))

        def mix(c):
            nc.scalar.copy(
                mixed[c][:].rearrange("p (c i) j -> p c j i", i=4),
                raw[c][:].rearrange("p j (c i) -> p c j i", i=4),
            )

        def quantise(c):
            nc.vector.quantize_mx(
                out=u_codes[c][:].bitcast(E4M3X4),
                scales=u_plane[c][:],
                in_=mixed[c][:].rearrange("p n j -> p (n j)"),
            )

        def table2(m):
            gather(got2[m], words2[m][:].bitcast(U32), list2)
            nc.vector.tensor_copy(
                part2[m][:].rearrange("p h b -> p (h b)").bitcast(U16).rearrange("p (h t) -> p h t", h=2),
                got2[m][:].bitcast(U16).rearrange("p (t h) -> p h t", h=2),
            )

        def u_pass(c, first):
            multiply(
                lambda n: u_codes[c][:, n * P : (n + 1) * P].bitcast(E4M3X4),
                u_plane[c],
                lambda h: part2[c // 2][:, c % 2, 2 * h * H : 2 * (h + 1) * H].bitcast(E2M1X4),
                gots2[c],
                first, False, None,
            )

        def w_pass(a, last):
            multiply(
                lambda n: w_codes[:, a, 2 * n * P : 2 * (n + 1) * P].bitcast(E2M1X4),
                w_plane[:, a, :],
                lambda h: got1[a][:, h * H : (h + 1) * H].bitcast(E4M3X4),
                gots1[a],
                False, last, None,
            )

        def table2_planes(m):
            for h in range(2):
                gather(gots2[2 * m + h], plane2[m][:, h, :], list2)

        def words_of_table1(a):
            gather(got1[a], words1[a][:].bitcast(U32), list1)

        nc.vector.memset(warm[:], 0.0)
        nc.scalar.activation(warm[:], warm[:], ACT.Silu)
        for a in range(KP):
            gather(gots1[a], plane1[:, a, :], list1)
        table2(0)
        table2_planes(0)
        mix(0)
        quantise(0)
        u_pass(0, True)
        table2(1)
        table2_planes(1)
        mix(1)
        quantise(1)
        u_pass(1, False)
        words_of_table1(0)
        nc.vector.transpose(bias[:], bias_rows[:])
        mix(2)
        quantise(2)
        u_pass(2, False)
        mix(3)
        quantise(3)
        u_pass(3, False)
        w_pass(0, False)
        words_of_table1(1)
        w_pass(1, False)
        for h in range(2):
            gather(got1[2], words1[2][:].bitcast(U32), list1, h * H, (h + 1) * H)
        w_pass(2, True)
        for h in range(2):
            for n in range(2):
                nc.scalar.activation(res[h][:, n, :], acc[n][h][:], ACT.Silu, bias=bias[:, 32 * n : 32 * n + 1])
                store = nc.sync if n == 0 else nc.scalar
                store.dma_start(out[n * P : (n + 1) * P, h * H : (h + 1) * H], res[h][:, n, :])
